import numpy as np
import ml_dtypes


def mxq(x, axis, fmt="e4m3"):
    dtype, down = {"e4m3": (ml_dtypes.float8_e4m3fn, 7), "e5m2": (ml_dtypes.float8_e5m2, 14)}[fmt]
    v = np.moveaxis(np.asarray(x, np.float32).astype(ml_dtypes.bfloat16).astype(np.float64), axis, -1)
    blocks = v.reshape(v.shape[:-1] + (-1, 32))
    amax = np.abs(blocks).max(-1, keepdims=True)
    byte = np.maximum(np.where(amax > 0, np.frexp(amax)[1] - 1 + 127, 0) - down, 1)
    scale = np.exp2(byte - 127.0)
    codes = (blocks / scale).astype(np.float32).astype(dtype).astype(np.float64)
    return np.moveaxis((codes * scale).reshape(v.shape), -1, axis)


WIDE = False


def mx_kscale(k):
    if not WIDE:
        return np.ones(k)
    levels = np.array([10, -10, 5, -5, 0])
    if k % 512:
        return np.exp2(np.random.permutation(np.resize(levels, k // 32))).repeat(32)
    a = np.empty((k // 512, 16))
    for p in range(k // 512):
        a[p, :8] = np.random.permutation(np.resize(levels, 8))
        for g in range(8):
            far = levels[np.abs(levels - a[p, g]) >= 10]
            a[p, g + 8] = far[np.random.randint(len(far))]
    return np.exp2(a.ravel()).repeat(32)


def f64(x):
    return np.asarray(x).astype(np.float64)


def striped(idx):
    return np.tile(idx.reshape(-1, 16).T, (8, 1)).astype(np.uint16)


def unstriped(offs):
    return offs[:16].T.reshape(-1).astype(np.int64)


def striped8(idx):
    return np.concatenate([x.reshape(-1, 16).T for x in idx]).astype(np.uint16)


def runs(offs, k):
    lists = np.stack([offs[16 * r : 16 * r + 16].T.reshape(-1) for r in range(8)]).astype(np.int64)
    return lists[np.arange(k) % 512 // 64]


def pack_weight(w):
    k, n = w.shape
    w = f64(np.asarray(w, np.float32).astype(ml_dtypes.bfloat16)).reshape(k // 32, 32, n)
    amax = np.abs(w).max(1)
    byte = np.clip(np.where(amax > 0, np.frexp(amax)[1] - 1 + 127 - 7, 1), 1, 254)
    scaled = (w * np.exp2(127.0 - byte)[:, None, :]).reshape(k, n).astype(np.float32)
    words = np.ascontiguousarray(scaled.reshape(k // 512, 128, 4, n).transpose(0, 1, 3, 2)).astype(ml_dtypes.float8_e4m3fn).view(np.uint8)
    return words, np.ascontiguousarray(byte.astype(np.uint8).reshape(k // 512, 16, n))


def unpack_weight(words, scales):
    g, p, n, _ = words.shape
    vals = np.ascontiguousarray(words).view(ml_dtypes.float8_e4m3fn).astype(np.float64) * np.repeat(np.exp2(scales.astype(np.float64) - 127.0), 8, axis=1)[..., None]
    return vals.transpose(0, 1, 3, 2).reshape(g * 512, n)


K, T, S, N, H = 512, 2048, 512, 512, 512


def setup_inputs():
    n = np.random.standard_normal
    s = mx_kscale(K)[:, None]
    u = mx_kscale(H)
    packed_xT = pack_weight(n((K, T)) * s)
    return {
        "x_words": packed_xT[0],
        "x_scales": packed_xT[1],
        "w1": (n((K, H)) / np.sqrt(K) / s).astype(np.float32),
        "gn": (np.random.uniform(0.5, 1.5, (H, 1)) * u[:, None]).astype(np.float32),
        "w2": (n((H, N)) / np.sqrt(H) / u[:, None]).astype(np.float32),
        "gm": (np.random.uniform(0.5, 1.5, (H, 1)) * u[:, None]).astype(np.float32),
        "w3": (n((H, N)) / np.sqrt(H) / u[:, None]).astype(np.float32),
        "offs": striped(np.random.permutation(T)[:S]),
        "n1": striped8(np.stack([np.random.permutation(S) for _ in range(8)])),
        "n2": striped8(np.stack([np.random.permutation(S) for _ in range(8)])),
        "n3": striped8(np.stack([np.random.permutation(S) for _ in range(8)])),
        "n4": striped8(np.stack([np.random.permutation(S) for _ in range(8)])),
        "n5": striped8(np.stack([np.random.permutation(S) for _ in range(8)])),
    }


def reference(x_words, x_scales, w1, gn, w2, gm, w3, offs, n1, n2, n3, n4, n5):
    xq = unpack_weight(x_words, x_scales)[:, unstriped(offs)]
    y = mxq(f64(w1), 0, "e4m3").T @ xq
    z = f64(gn) * (np.maximum(y, y[np.arange(H)[:, None], runs(n1, H)]))
    a = mxq(f64(w2), 0, "e4m3").T @ mxq(z, 0, "e4m3")
    ex = np.exp(0.5 * y)
    z2 = f64(gm) * ((2.0 * ex) / (ex + ex[np.arange(H)[:, None], runs(n2, H)] + ex[np.arange(H)[:, None], runs(n3, H)]))
    b = mxq(f64(w3), 0, "e4m3").T @ mxq(z2, 0, "e4m3")
    return a[np.arange(N)[:, None], runs(n4, N)] - (np.tanh(b) * (b[np.arange(N)[:, None], runs(n5, N)]))

@@ -1,0 +1,234 @@
+from contextlib import ExitStack
+
+import concourse.mybir as mybir
+from concourse.masks import make_identity
+
+K, T, S, H, N = 512, 2048, 512, 512, 512
+FLOPS = 2 * S * (K * H + 2 * H * N)
+
+F32 = mybir.dt.float32
+BF16 = mybir.dt.bfloat16
+I32 = mybir.dt.int32
+U32 = mybir.dt.uint32
+U16 = mybir.dt.uint16
+U8 = mybir.dt.uint8
+FP8X4 = mybir.dt.float8_e4m3fn_x4
+ACT = mybir.ActivationFunctionType
+ALU = mybir.AluOpType
+
+P = 128
+PACK = 4
+HALF = S // 2
+LIST_COLS = S // 16
+
+
+def tile_picked_forksoftbbigshare_none_p_kernel(
+    tc, x_words, x_scales, w1, gn, w2, gm, w3, offs, n1, n2, n3, n4, n5, out
+):
+    nc = tc.nc
+    planes = range(PACK)
+    halves = range(2)
+
+    def cols(c):
+        return slice(c * HALF, (c + 1) * HALF)
+
+    def entries(lst, c):
+        return lst[:, c * LIST_COLS // 2 : (c + 1) * LIST_COLS // 2]
+
+    with ExitStack() as ctx:
+        sb = ctx.enter_context(tc.tile_pool(name="sb", bufs=1))
+        ps = ctx.enter_context(tc.psum_pool(name="ps", bufs=1))
+
+        def load_list(name, src):
+            lst = sb.tile([P, LIST_COLS], U16, name=name)
+            nc.sync.dma_start(lst[:], src)
+            return lst
+
+        def load_weight(name, w):
+            raw = sb.tile([P, PACK, N], F32, name=name)
+            nc.sync.dma_start(raw[:], w.rearrange("(p j) n -> p j n", j=PACK))
+            return raw
+
+        def load_gain(name, g):
+            raw = sb.tile([P, PACK], F32, name=name)
+            nc.scalar.dma_start(raw[:], g.rearrange("(p t) o -> p (t o)", t=PACK))
+            return raw
+
+        def mx_tiles(name, width):
+            codes = sb.tile([P, width], U32, name=name + "_codes", align_bytes=64)
+            scales = sb.tile([P, width], U8, name=name + "_scales", align_bytes=64)
+            return codes, scales
+
+        def round_weight(name, raw):
+            grouped = sb.tile([P, N * PACK], BF16, name=name, align_bytes=64)
+            nc.vector.tensor_copy(
+                grouped[:].rearrange("p (t m j) -> p m j t", t=PACK, j=PACK),
+                raw[:].rearrange("p j (m t) -> p m j t", t=PACK),
+            )
+            return grouped
+
+        def quantize(mx, grouped, sl):
+            nc.vector.quantize_mx(out=mx[0][:, sl].bitcast(FP8X4), scales=mx[1][:, sl], in_=grouped)
+
+        def product(acc, w_mx, t, x_mx, sl):
+            rows = slice(t * P, (t + 1) * P)
+            nc.tensor.matmul_mx(
+                out=acc,
+                lhsT=w_mx[0][:, rows].bitcast(FP8X4),
+                lhsT_scale=w_mx[1][:, rows],
+                rhs=x_mx[0][:, sl].bitcast(FP8X4),
+                rhs_scale=x_mx[1][:, sl],
+                start=True,
+                stop=True,
+            )
+
+        def gain_and_interleave(name, src, gain, sl):
+            width = sl.stop - sl.start
+            grouped = sb.tile([P, width * PACK], BF16, name=name, align_bytes=64)
+            nc.vector.tensor_tensor(
+                grouped[:].rearrange("p (c i t) -> p c t i", i=4, t=PACK),
+                src[:, :, sl].rearrange("p t (c i) -> p c t i", i=4),
+                gain[:].unsqueeze(1).unsqueeze(3).to_broadcast([P, width // 4, PACK, 4]),
+                ALU.mult,
+            )
+            return grouped
+
+        xs_all = sb.tile([P, T], U8, name="xs_all")
+        nc.vector.memset(xs_all[:].bitcast(I32), 0)
+        offs_sb = load_list("offs_sb", offs)
+        w1_raw = load_weight("w1_raw", w1)
+        for q in range(4):
+            nc.scalar.dma_start(
+                xs_all[32 * q : 32 * q + 4, :].bitcast(I32), x_scales[0, 4 * q : 4 * q + 4, :].bitcast(I32)
+            )
+        xw_all = sb.tile([P, T], I32, name="xw_all")
+        nc.sync.dma_start(xw_all[:], x_words[0].rearrange("p n r -> p (n r)").bitcast(I32))
+        n2_sb = load_list("n2_sb", n2)
+        n3_sb = load_list("n3_sb", n3)
+        n1_sb = load_list("n1_sb", n1)
+        gn_raw = load_gain("gn_raw", gn)
+        gm_raw = load_gain("gm_raw", gm)
+        w3_raw = load_weight("w3_raw", w3)
+        w2_raw = load_weight("w2_raw", w2)
+        n5_sb = load_list("n5_sb", n5)
+        n4_sb = load_list("n4_sb", n4)
+
+        ident = sb.tile([P, P], F32, name="ident")
+        make_identity(nc, ident[:])
+        gn2 = sb.tile([P, PACK], F32, name="gn2")
+        gm2 = sb.tile([P, PACK], F32, name="gm2")
+        nc.scalar.activation(gn2[:], gn_raw[:], ACT.Copy, scale=2.0)
+        nc.scalar.activation(gm2[:], gm_raw[:], ACT.Copy, scale=2.0)
+
+        def bank(name, number, shape):
+            return ps.tile(shape, F32, name=name, tag="bank%d" % number)
+
+        x_mx = mx_tiles("x", S)
+        w1_mx = mx_tiles("w1", H)
+        w1_bf = round_weight("w1_bf", w1_raw)
+        nc.vector.tensor_copy(x_mx[1][:], xs_all[:].indirect(offs_sb[:]))
+        quantize(w1_mx, w1_bf[:], slice(0, H))
+        nc.vector.tensor_copy(x_mx[0][:], xw_all[:].bitcast(U32).indirect(offs_sb[:]))
+
+        h = [sb.tile([P, S], F32, name="half_y%d" % t) for t in planes]
+        for t in planes:
+            acc = bank("y_acc%d" % t, t, [P, S])
+            product(acc[:], w1_mx, t, x_mx, slice(0, S))
+            if t == 0:
+                nc.scalar.activation(h[t][:], acc[:], ACT.Copy, scale=0.5)
+            else:
+                nc.vector.tensor_scalar(h[t][:], acc[:], 0.5, None, ALU.mult)
+
+        ex23_t = []
+        for t in planes:
+            ex2 = sb.tile([P, S], F32, name="ex2_%d" % t)
+            ex3 = sb.tile([P, S], F32, name="ex3_%d" % t)
+            sums = bank("ex23_t%d" % t, t, [P, PACK, P])
+            for c in halves:
+                nc.scalar.activation(ex2[:, cols(c)], h[t][:].indirect(entries(n2_sb, c)), ACT.Exp)
+            for c in halves:
+                nc.scalar.activation(ex3[:, cols(c)], h[t][:].indirect(entries(n3_sb, c)), ACT.Exp)
+            for blk in range(S // P):
+                for first, ex in ((True, ex2), (False, ex3)):
+                    nc.tensor.matmul(
+                        sums[:, blk, :], ex[:, blk * P : (blk + 1) * P], ident[:],
+                        start=first, stop=not first, is_transpose=True,
+                    )
+            ex23_t.append(sums)
+
+        w3_mx = mx_tiles("w3", N)
+        w3_bf = round_weight("w3_bf", w3_raw)
+        quantize(w3_mx, w3_bf[:], slice(0, N))
+
+        h1 = sb.tile([P, PACK, S], F32, name="h1")
+        hmax = sb.tile([P, PACK, S], F32, name="hmax")
+        for t in planes:
+            for c in halves:
+                nc.vector.tensor_copy(h1[:, t, cols(c)], h[t][:].indirect(entries(n1_sb, c)))
+            if t > 0:
+                nc.vector.tensor_tensor(hmax[:, t - 1, :], h1[:, t - 1, :], h[t - 1][:], ALU.max)
+        w2_bf = round_weight("w2_bf", w2_raw)
+        nc.vector.tensor_tensor(hmax[:, PACK - 1, :], h1[:, PACK - 1, :], h[PACK - 1][:], ALU.max)
+        w2_mx = mx_tiles("w2", N)
+        quantize(w2_mx, w2_bf[:], slice(0, N))
+        z_mx = mx_tiles("z", S)
+        z_bf = [gain_and_interleave("z_bf%d" % c, hmax, gn2, cols(c)) for c in halves]
+
+        logit = sb.tile([P, PACK, S], F32, name="logit")
+        share = sb.tile([P, PACK, S], F32, name="share")
+        for t in planes:
+            lse_t = sb.tile([P, PACK, P], F32, name="lse_t%d" % t)
+            nc.scalar.activation(lse_t[:], ex23_t[t][:], ACT.Ln)
+            lse = bank("lse%d" % t, PACK + t, [P, S])
+            for blk in range(S // P):
+                nc.tensor.transpose(lse[:, blk * P : (blk + 1) * P], lse_t[:, blk, :], ident[:])
+            nc.vector.tensor_tensor(logit[:, t, :], h[t][:], lse[:], ALU.subtract)
+
+        for c in halves:
+            quantize(z_mx, z_bf[c][:], cols(c))
+        a_acc = [bank("a_acc%d" % t, PACK + t, [P, S]) for t in planes]
+        for t in planes:
+            product(a_acc[t][:], w2_mx, t, z_mx, slice(0, S))
+
+        pieces = [slice(0, 256), slice(256, 384), slice(384, 512)]
+        for sl in pieces:
+            nc.scalar.activation(share[:, :, sl], logit[:, :, sl], ACT.Sigmoid)
+        z2_bf = [gain_and_interleave("z2_bf0", share, gm2, pieces[0])]
+        b_acc = {}
+        b_banks = []
+        for c, sl in enumerate(pieces):
+            width = sl.stop - sl.start
+            if c + 1 < len(pieces):
+                z2_bf.append(gain_and_interleave("z2_bf%d" % (c + 1), share, gm2, pieces[c + 1]))
+            z2_mx = mx_tiles("z2_%d" % c, width)
+            quantize(z2_mx, z2_bf[c][:], slice(0, width))
+            per_bank = S // width
+            for t0 in range(0, PACK, per_bank):
+                acc = bank("b_acc%d%d" % (c, t0), len(b_banks), [P, per_bank, width])
+                b_banks.append((acc, t0, per_bank, sl))
+                for e in range(per_bank):
+                    product(acc[:, e, :], w3_mx, t0 + e, z2_mx, slice(0, width))
+                    b_acc[c, t0 + e] = acc[:, e, :]
+
+        tanh_b = sb.tile([P, PACK, S], F32, name="tanh_b")
+        prod = sb.tile([P, PACK, S], F32, name="prod")
+        out_rows = out.rearrange("(p t) n -> p t n", t=PACK)
+        for t in planes:
+            a = sb.tile([P, S], F32, name="a%d" % t)
+            b = sb.tile([P, S], F32, name="b%d" % t)
+            res = sb.tile([P, S], F32, name="res%d" % t)
+            for c, sl in enumerate(pieces):
+                nc.scalar.copy(b[:, sl], b_acc[c, t])
+            for acc, t0, per_bank, sl in b_banks:
+                if t0 == t:
+                    nc.scalar.activation(tanh_b[:, t0 : t0 + per_bank, sl], acc[:], ACT.Tanh)
+            nc.scalar.copy(a[:], a_acc[t][:])
+            for c in halves:
+                nc.vector.tensor_tensor(
+                    prod[:, t, cols(c)], b[:].indirect(entries(n5_sb, c)), tanh_b[:, t, cols(c)], ALU.mult
+                )
+            for c in halves:
+                nc.vector.tensor_tensor(
+                    res[:, cols(c)], a[:].indirect(entries(n4_sb, c)), prod[:, t, cols(c)], ALU.subtract
+                )
+            nc.sync.dma_start(out_rows[:, t, :], res[:])

@@ -128,47 +128,55 @@ def tile_picked_forksoftbbigshare_none_p_kernel(
         w1_bf = round_weight("w1_bf", w1_raw)
         nc.vector.tensor_copy(x_mx[1][:], xs_all[:].indirect(offs_sb[:]))
         quantize(w1_mx, w1_bf[:], slice(0, H))
-        nc.vector.tensor_copy(x_mx[0][:], xw_all[:].bitcast(U32).indirect(offs_sb[:]))
+        for c in halves:
+            nc.vector.tensor_copy(x_mx[0][:, cols(c)], xw_all[:].bitcast(U32).indirect(entries(offs_sb, c)))
 
-        h = [sb.tile([P, S], F32, name="half_y%d" % t) for t in planes]
+        h_win = [sb.tile([P, 2 * S], F32, name="half_y%d" % t) for t in planes]
         for t in planes:
-            acc = bank("y_acc%d" % t, t, [P, S])
-            product(acc[:], w1_mx, t, x_mx, slice(0, S))
-            if t == 0:
-                nc.scalar.activation(h[t][:], acc[:], ACT.Copy, scale=0.5)
-            else:
-                nc.vector.tensor_scalar(h[t][:], acc[:], 0.5, None, ALU.mult)
+            nc.gpsimd.memset(h_win[t][:, S:], 0.0)
+        h = [h_win[t][:, :S] for t in planes]
+        for c in halves:
+            for u in range(2):
+                acc = bank("y_acc%d%d" % (c, u), 2 * c + u, [P, 2, HALF])
+                for e in range(2):
+                    product(acc[:, e, :], w1_mx, 2 * u + e, x_mx, cols(c))
+                for e in range(2):
+                    t = 2 * u + e
+                    if t == 0 or (c == 0 and u == 0):
+                        nc.scalar.activation(h[t][:, cols(c)], acc[:, e, :], ACT.Copy, scale=0.5)
+                    else:
+                        nc.vector.tensor_scalar(h[t][:, cols(c)], acc[:, e, :], 0.5, None, ALU.mult)
 
         ex23_t = []
+        ex_win = []
         for t in planes:
-            ex2 = sb.tile([P, S], F32, name="ex2_%d" % t)
-            ex3 = sb.tile([P, S], F32, name="ex3_%d" % t)
-            sums = bank("ex23_t%d" % t, t, [P, PACK, P])
-            for c in halves:
-                nc.scalar.activation(ex2[:, cols(c)], h[t][:].indirect(entries(n2_sb, c)), ACT.Exp)
-            for c in halves:
-                nc.scalar.activation(ex3[:, cols(c)], h[t][:].indirect(entries(n3_sb, c)), ACT.Exp)
+            ex = sb.tile([P, 2 * S], F32, name="ex_%d" % t)
+            ex_win.append(ex)
+            sums = bank("ex23_t%d" % t, PACK + t, [P, PACK, P])
+            nc.scalar.activation(ex[:, :S], h_win[t][:].indirect(n2_sb[:]), ACT.Exp)
+            nc.scalar.activation(ex[:, S:], h_win[t][:].indirect(n3_sb[:]), ACT.Exp)
             for blk in range(S // P):
-                for first, ex in ((True, ex2), (False, ex3)):
+                for term in range(2):
+                    start = term * S + blk * P
                     nc.tensor.matmul(
-                        sums[:, blk, :], ex[:, blk * P : (blk + 1) * P], ident[:],
-                        start=first, stop=not first, is_transpose=True,
+                        sums[:, blk, :], ex[:, start : start + P], ident[:],
+                        start=term == 0, stop=term == 1, is_transpose=True,
                     )
             ex23_t.append(sums)
 
         w3_mx = mx_tiles("w3", N)
         w3_bf = round_weight("w3_bf", w3_raw)
-        quantize(w3_mx, w3_bf[:], slice(0, N))
 
         h1 = sb.tile([P, PACK, S], F32, name="h1")
         hmax = sb.tile([P, PACK, S], F32, name="hmax")
         for t in planes:
-            for c in halves:
-                nc.vector.tensor_copy(h1[:, t, cols(c)], h[t][:].indirect(entries(n1_sb, c)))
+            nc.vector.tensor_copy(h1[:, t, :], h_win[t][:].indirect(n1_sb[:]))
+            if t == 0:
+                quantize(w3_mx, w3_bf[:], slice(0, N))
             if t > 0:
-                nc.vector.tensor_tensor(hmax[:, t - 1, :], h1[:, t - 1, :], h[t - 1][:], ALU.max)
+                nc.vector.tensor_tensor(hmax[:, t - 1, :], h1[:, t - 1, :], h[t - 1], ALU.max)
         w2_bf = round_weight("w2_bf", w2_raw)
-        nc.vector.tensor_tensor(hmax[:, PACK - 1, :], h1[:, PACK - 1, :], h[PACK - 1][:], ALU.max)
+        nc.vector.tensor_tensor(hmax[:, PACK - 1, :], h1[:, PACK - 1, :], h[PACK - 1], ALU.max)
         w2_mx = mx_tiles("w2", N)
         quantize(w2_mx, w2_bf[:], slice(0, N))
         z_mx = mx_tiles("z", S)
@@ -179,10 +187,10 @@ def tile_picked_forksoftbbigshare_none_p_kernel(
         for t in planes:
             lse_t = sb.tile([P, PACK, P], F32, name="lse_t%d" % t)
             nc.scalar.activation(lse_t[:], ex23_t[t][:], ACT.Ln)
-            lse = bank("lse%d" % t, PACK + t, [P, S])
+            lse = bank("lse%d" % t, t, [P, S])
             for blk in range(S // P):
                 nc.tensor.transpose(lse[:, blk * P : (blk + 1) * P], lse_t[:, blk, :], ident[:])
-            nc.vector.tensor_tensor(logit[:, t, :], h[t][:], lse[:], ALU.subtract)
+            nc.vector.tensor_tensor(logit[:, t, :], h[t], lse[:], ALU.subtract)
 
         for c in halves:
             quantize(z_mx, z_bf[c][:], cols(c))
@@ -190,9 +198,11 @@ def tile_picked_forksoftbbigshare_none_p_kernel(
         for t in planes:
             product(a_acc[t][:], w2_mx, t, z_mx, slice(0, S))
 
-        pieces = [slice(0, 256), slice(256, 384), slice(384, 512)]
+        pieces = [slice(0, 128), slice(128, 384), slice(384, 512)]
         for sl in pieces:
             nc.scalar.activation(share[:, :, sl], logit[:, :, sl], ACT.Sigmoid)
+        a_win = ex_win
+        nc.scalar.copy(a_win[0][:, :S], a_acc[0][:])
         z2_bf = [gain_and_interleave("z2_bf0", share, gm2, pieces[0])]
         b_acc = {}
         b_banks = []
@@ -210,25 +220,32 @@ def tile_picked_forksoftbbigshare_none_p_kernel(
                     product(acc[:, e, :], w3_mx, t0 + e, z2_mx, slice(0, width))
                     b_acc[c, t0 + e] = acc[:, e, :]
 
+        b_win = h_win
+        a4_first = sb.tile([P, S], F32, name="a4_first")
+        nc.vector.tensor_copy(a4_first[:], a_win[0][:].indirect(n4_sb[:]))
         tanh_b = sb.tile([P, PACK, S], F32, name="tanh_b")
         prod = sb.tile([P, PACK, S], F32, name="prod")
         out_rows = out.rearrange("(p t) n -> p t n", t=PACK)
-        for t in planes:
-            a = sb.tile([P, S], F32, name="a%d" % t)
-            b = sb.tile([P, S], F32, name="b%d" % t)
-            res = sb.tile([P, S], F32, name="res%d" % t)
+
+        def multiply(t):
             for c, sl in enumerate(pieces):
-                nc.scalar.copy(b[:, sl], b_acc[c, t])
+                nc.scalar.copy(b_win[t][:, sl], b_acc[c, t])
             for acc, t0, per_bank, sl in b_banks:
                 if t0 == t:
                     nc.scalar.activation(tanh_b[:, t0 : t0 + per_bank, sl], acc[:], ACT.Tanh)
-            nc.scalar.copy(a[:], a_acc[t][:])
+            nc.vector.tensor_tensor(prod[:, t, :], b_win[t][:].indirect(n5_sb[:]), tanh_b[:, t, :], ALU.mult)
+
+        def subtract_and_store(t):
+            if t > 0:
+                nc.scalar.copy(a_win[t][:, :S], a_acc[t][:])
+            res = sb.tile([P, S], F32, name="res%d" % t)
             for c in halves:
-                nc.vector.tensor_tensor(
-                    prod[:, t, cols(c)], b[:].indirect(entries(n5_sb, c)), tanh_b[:, t, cols(c)], ALU.mult
-                )
-            for c in halves:
-                nc.vector.tensor_tensor(
-                    res[:, cols(c)], a[:].indirect(entries(n4_sb, c)), prod[:, t, cols(c)], ALU.subtract
-                )
-            nc.sync.dma_start(out_rows[:, t, :], res[:])
+                a4 = a4_first[:, cols(c)] if t == 0 else a_win[t][:].indirect(entries(n4_sb, c))
+                nc.vector.tensor_tensor(res[:, cols(c)], a4, prod[:, t, cols(c)], ALU.subtract)
+                nc.sync.dma_start(out_rows[:, t, cols(c)], res[:, cols(c)])
+
+        multiply(0)
+        for t in planes:
+            if t + 1 < PACK:
+                multiply(t + 1)
+            subtract_and_store(t)

@@ -114,7 +114,8 @@ def tile_picked_forksoftbbigshare_none_p_kernel(
         n4_sb = load_list("n4_sb", n4)
 
         ident = sb.tile([P, P], F32, name="ident")
-        make_identity(nc, ident[:])
+        nc.vector.memset(ident[:], 0.0)
+        make_identity(nc, ident[:], nomemset=True)
         gn2 = sb.tile([P, PACK], F32, name="gn2")
         gm2 = sb.tile([P, PACK], F32, name="gm2")
         nc.scalar.activation(gn2[:], gn_raw[:], ACT.Copy, scale=2.0)
@@ -133,7 +134,7 @@ def tile_picked_forksoftbbigshare_none_p_kernel(
 
         h_win = [sb.tile([P, 2 * S], F32, name="half_y%d" % t) for t in planes]
         for t in planes:
-            nc.gpsimd.memset(h_win[t][:, S:], 0.0)
+            nc.vector.memset(h_win[t][:, S:], 0.0)
         h = [h_win[t][:, :S] for t in planes]
         for c in halves:
             for u in range(2):

@@ -62,8 +62,8 @@ def tile_picked_forksoftbbigshare_none_p_kernel(
         def round_weight(name, raw):
             grouped = sb.tile([P, N * PACK], BF16, name=name, align_bytes=64)
             nc.vector.tensor_copy(
-                grouped[:].rearrange("p (t m j) -> p m j t", t=PACK, j=PACK),
-                raw[:].rearrange("p j (m t) -> p m j t", t=PACK),
+                grouped[:].rearrange("p (t q i j) -> p t q i j", t=PACK, i=8, j=PACK),
+                raw[:].rearrange("p j (q t i) -> p t q i j", t=PACK, i=8),
             )
             return grouped
 
@@ -126,9 +126,13 @@ def tile_picked_forksoftbbigshare_none_p_kernel(
 
         x_mx = mx_tiles("x", S)
         w1_mx = mx_tiles("w1", H)
-        w1_bf = round_weight("w1_bf", w1_raw)
+        w1_cols = w1_raw[:].rearrange("p j (m t) -> p t m j", t=PACK)
+        w1_bf = [sb.tile([P, 2, P, PACK], BF16, name="w1_bf%d" % u, align_bytes=64) for u in range(2)]
+        nc.vector.tensor_copy(w1_bf[0][:], w1_cols[:, 0:2])
+        nc.scalar.copy(w1_bf[1][:], w1_cols[:, 2:4])
         nc.vector.tensor_copy(x_mx[1][:], xs_all[:].indirect(offs_sb[:]))
-        quantize(w1_mx, w1_bf[:], slice(0, H))
+        for u in range(2):
+            quantize(w1_mx, w1_bf[u][:].rearrange("p t m j -> p (t m j)"), slice(2 * u * P, 2 * (u + 1) * P))
         for c in halves:
             nc.vector.tensor_copy(x_mx[0][:, cols(c)], xw_all[:].bitcast(U32).indirect(entries(offs_sb, c)))
 
@@ -226,7 +230,7 @@ def tile_picked_forksoftbbigshare_none_p_kernel(
         nc.vector.tensor_copy(a4_first[:], a_win[0][:].indirect(n4_sb[:]))
         tanh_b = sb.tile([P, PACK, S], F32, name="tanh_b")
         prod = sb.tile([P, PACK, S], F32, name="prod")
-        out_rows = out.rearrange("(p t) n -> p t n", t=PACK)
+        out_rows = out.rearrange("(q t i) n -> t q i n", t=PACK, i=8)
 
         def multiply(t):
             for c, sl in enumerate(pieces):
@@ -243,7 +247,7 @@ def tile_picked_forksoftbbigshare_none_p_kernel(
             for c in halves:
                 a4 = a4_first[:, cols(c)] if t == 0 else a_win[t][:].indirect(entries(n4_sb, c))
                 nc.vector.tensor_tensor(res[:, cols(c)], a4, prod[:, t, cols(c)], ALU.subtract)
-                nc.sync.dma_start(out_rows[:, t, cols(c)], res[:, cols(c)])
+                nc.sync.dma_start(out_rows[t, :, :, cols(c)], res[:, cols(c)])
 
         multiply(0)
         for t in planes:

from contextlib import ExitStack

import concourse.mybir as mybir
from concourse.masks import make_identity

K, T, S, H, N = 512, 2048, 512, 512, 512
FLOPS = 2 * S * (K * H + 2 * H * N)

F32 = mybir.dt.float32
BF16 = mybir.dt.bfloat16
I32 = mybir.dt.int32
U32 = mybir.dt.uint32
U16 = mybir.dt.uint16
U8 = mybir.dt.uint8
FP8X4 = mybir.dt.float8_e4m3fn_x4
ACT = mybir.ActivationFunctionType
ALU = mybir.AluOpType

P = 128
PACK = 4
HALF = S // 2
LIST_COLS = S // 16


def tile_picked_forksoftbbigshare_none_p_kernel(
    tc, x_words, x_scales, w1, gn, w2, gm, w3, offs, n1, n2, n3, n4, n5, out
):
    nc = tc.nc
    planes = range(PACK)
    halves = range(2)

    def cols(c):
        return slice(c * HALF, (c + 1) * HALF)

    def entries(lst, c):
        return lst[:, c * LIST_COLS // 2 : (c + 1) * LIST_COLS // 2]

    with ExitStack() as ctx:
        sb = ctx.enter_context(tc.tile_pool(name="sb", bufs=1))
        ps = ctx.enter_context(tc.psum_pool(name="ps", bufs=1))

        def load_list(name, src):
            lst = sb.tile([P, LIST_COLS], U16, name=name)
            nc.sync.dma_start(lst[:], src)
            return lst

        def load_weight(name, w):
            raw = sb.tile([P, PACK, N], F32, name=name)
            nc.sync.dma_start(raw[:], w.rearrange("(p j) n -> p j n", j=PACK))
            return raw

        def load_gain(name, g):
            raw = sb.tile([P, PACK], F32, name=name)
            nc.scalar.dma_start(raw[:], g.rearrange("(p t) o -> p (t o)", t=PACK))
            return raw

        def mx_tiles(name, width):
            codes = sb.tile([P, width], U32, name=name + "_codes", align_bytes=64)
            scales = sb.tile([P, width], U8, name=name + "_scales", align_bytes=64)
            return codes, scales

        def round_weight(name, raw):
            grouped = sb.tile([P, N * PACK], BF16, name=name, align_bytes=64)
            nc.vector.tensor_copy(
                grouped[:].rearrange("p (t q i j) -> p t q i j", t=PACK, i=8, j=PACK),
                raw[:].rearrange("p j (q t i) -> p t q i j", t=PACK, i=8),
            )
            return grouped

        def quantize(mx, grouped, sl):
            nc.vector.quantize_mx(out=mx[0][:, sl].bitcast(FP8X4), scales=mx[1][:, sl], in_=grouped)

        def product(acc, w_mx, t, x_mx, sl):
            rows = slice(t * P, (t + 1) * P)
            nc.tensor.matmul_mx(
                out=acc,
                lhsT=w_mx[0][:, rows].bitcast(FP8X4),
                lhsT_scale=w_mx[1][:, rows],
                rhs=x_mx[0][:, sl].bitcast(FP8X4),
                rhs_scale=x_mx[1][:, sl],
                start=True,
                stop=True,
            )

        def gain_and_interleave(name, src, gain, sl):
            width = sl.stop - sl.start
            grouped = sb.tile([P, width * PACK], BF16, name=name, align_bytes=64)
            nc.vector.tensor_tensor(
                grouped[:].rearrange("p (c i t) -> p c t i", i=4, t=PACK),
                src[:, :, sl].rearrange("p t (c i) -> p c t i", i=4),
                gain[:].unsqueeze(1).unsqueeze(3).to_broadcast([P, width // 4, PACK, 4]),
                ALU.mult,
            )
            return grouped

        xs_all = sb.tile([P, T], U8, name="xs_all")
        nc.vector.memset(xs_all[:].bitcast(I32), 0)
        offs_sb = load_list("offs_sb", offs)
        w1_raw = load_weight("w1_raw", w1)
        for q in range(4):
            nc.scalar.dma_start(
                xs_all[32 * q : 32 * q + 4, :].bitcast(I32), x_scales[0, 4 * q : 4 * q + 4, :].bitcast(I32)
            )
        xw_all = sb.tile([P, T], I32, name="xw_all")
        nc.sync.dma_start(xw_all[:], x_words[0].rearrange("p n r -> p (n r)").bitcast(I32))
        n2_sb = load_list("n2_sb", n2)
        n3_sb = load_list("n3_sb", n3)
        n1_sb = load_list("n1_sb", n1)
        gn_raw = load_gain("gn_raw", gn)
        gm_raw = load_gain("gm_raw", gm)
        w3_raw = load_weight("w3_raw", w3)
        w2_raw = load_weight("w2_raw", w2)
        n5_sb = load_list("n5_sb", n5)
        n4_sb = load_list("n4_sb", n4)

        ident = sb.tile([P, P], F32, name="ident")
        nc.vector.memset(ident[:], 0.0)
        make_identity(nc, ident[:], nomemset=True)
        gn2 = sb.tile([P, PACK], F32, name="gn2")
        gm2 = sb.tile([P, PACK], F32, name="gm2")
        nc.scalar.activation(gn2[:], gn_raw[:], ACT.Copy, scale=2.0)
        nc.scalar.activation(gm2[:], gm_raw[:], ACT.Copy, scale=2.0)

        def bank(name, number, shape):
            return ps.tile(shape, F32, name=name, tag="bank%d" % number)

        x_mx = mx_tiles("x", S)
        w1_mx = mx_tiles("w1", H)
        w1_cols = w1_raw[:].rearrange("p j (m t) -> p t m j", t=PACK)
        w1_bf = [sb.tile([P, 2, P, PACK], BF16, name="w1_bf%d" % u, align_bytes=64) for u in range(2)]
        nc.vector.tensor_copy(w1_bf[0][:], w1_cols[:, 0:2])
        nc.scalar.copy(w1_bf[1][:], w1_cols[:, 2:4])
        nc.vector.tensor_copy(x_mx[1][:], xs_all[:].indirect(offs_sb[:]))
        for u in range(2):
            quantize(w1_mx, w1_bf[u][:].rearrange("p t m j -> p (t m j)"), slice(2 * u * P, 2 * (u + 1) * P))
        for c in halves:
            nc.vector.tensor_copy(x_mx[0][:, cols(c)], xw_all[:].bitcast(U32).indirect(entries(offs_sb, c)))

        h_win = [sb.tile([P, 2 * S], F32, name="half_y%d" % t) for t in planes]
        for t in planes:
            nc.vector.memset(h_win[t][:, S:], 0.0)
        h = [h_win[t][:, :S] for t in planes]
        for c in halves:
            for u in range(2):
                acc = bank("y_acc%d%d" % (c, u), 2 * c + u, [P, 2, HALF])
                for e in range(2):
                    product(acc[:, e, :], w1_mx, 2 * u + e, x_mx, cols(c))
                for e in range(2):
                    t = 2 * u + e
                    if t == 0 or (c == 0 and u == 0):
                        nc.scalar.activation(h[t][:, cols(c)], acc[:, e, :], ACT.Copy, scale=0.5)
                    else:
                        nc.vector.tensor_scalar(h[t][:, cols(c)], acc[:, e, :], 0.5, None, ALU.mult)

        ex23_t = []
        ex_win = []
        for t in planes:
            ex = sb.tile([P, 2 * S], F32, name="ex_%d" % t)
            ex_win.append(ex)
            sums = bank("ex23_t%d" % t, PACK + t, [P, PACK, P])
            nc.scalar.activation(ex[:, :S], h_win[t][:].indirect(n2_sb[:]), ACT.Exp)
            nc.scalar.activation(ex[:, S:], h_win[t][:].indirect(n3_sb[:]), ACT.Exp)
            for blk in range(S // P):
                for term in range(2):
                    start = term * S + blk * P
                    nc.tensor.matmul(
                        sums[:, blk, :], ex[:, start : start + P], ident[:],
                        start=term == 0, stop=term == 1, is_transpose=True,
                    )
            ex23_t.append(sums)

        w3_mx = mx_tiles("w3", N)
        w3_bf = round_weight("w3_bf", w3_raw)

        h1 = sb.tile([P, PACK, S], F32, name="h1")
        hmax = sb.tile([P, PACK, S], F32, name="hmax")
        for t in planes:
            nc.vector.tensor_copy(h1[:, t, :], h_win[t][:].indirect(n1_sb[:]))
            if t == 0:
                quantize(w3_mx, w3_bf[:], slice(0, N))
            if t > 0:
                nc.vector.tensor_tensor(hmax[:, t - 1, :], h1[:, t - 1, :], h[t - 1], ALU.max)
        w2_bf = round_weight("w2_bf", w2_raw)
        nc.vector.tensor_tensor(hmax[:, PACK - 1, :], h1[:, PACK - 1, :], h[PACK - 1], ALU.max)
        w2_mx = mx_tiles("w2", N)
        quantize(w2_mx, w2_bf[:], slice(0, N))
        z_mx = mx_tiles("z", S)
        z_bf = [gain_and_interleave("z_bf%d" % c, hmax, gn2, cols(c)) for c in halves]

        logit = sb.tile([P, PACK, S], F32, name="logit")
        share = sb.tile([P, PACK, S], F32, name="share")
        for t in planes:
            lse_t = sb.tile([P, PACK, P], F32, name="lse_t%d" % t)
            nc.scalar.activation(lse_t[:], ex23_t[t][:], ACT.Ln)
            lse = bank("lse%d" % t, t, [P, S])
            for blk in range(S // P):
                nc.tensor.transpose(lse[:, blk * P : (blk + 1) * P], lse_t[:, blk, :], ident[:])
            nc.vector.tensor_tensor(logit[:, t, :], h[t], lse[:], ALU.subtract)

        for c in halves:
            quantize(z_mx, z_bf[c][:], cols(c))
        a_acc = [bank("a_acc%d" % t, PACK + t, [P, S]) for t in planes]
        for t in planes:
            product(a_acc[t][:], w2_mx, t, z_mx, slice(0, S))

        pieces = [slice(0, 128), slice(128, 384), slice(384, 512)]
        for sl in pieces:
            nc.scalar.activation(share[:, :, sl], logit[:, :, sl], ACT.Sigmoid)
        a_win = ex_win
        nc.scalar.copy(a_win[0][:, :S], a_acc[0][:])
        z2_bf = [gain_and_interleave("z2_bf0", share, gm2, pieces[0])]
        b_acc = {}
        b_banks = []
        for c, sl in enumerate(pieces):
            width = sl.stop - sl.start
            if c + 1 < len(pieces):
                z2_bf.append(gain_and_interleave("z2_bf%d" % (c + 1), share, gm2, pieces[c + 1]))
            z2_mx = mx_tiles("z2_%d" % c, width)
            quantize(z2_mx, z2_bf[c][:], slice(0, width))
            per_bank = S // width
            for t0 in range(0, PACK, per_bank):
                acc = bank("b_acc%d%d" % (c, t0), len(b_banks), [P, per_bank, width])
                b_banks.append((acc, t0, per_bank, sl))
                for e in range(per_bank):
                    product(acc[:, e, :], w3_mx, t0 + e, z2_mx, slice(0, width))
                    b_acc[c, t0 + e] = acc[:, e, :]

        b_win = h_win
        a4_first = sb.tile([P, S], F32, name="a4_first")
        nc.vector.tensor_copy(a4_first[:], a_win[0][:].indirect(n4_sb[:]))
        tanh_b = sb.tile([P, PACK, S], F32, name="tanh_b")
        prod = sb.tile([P, PACK, S], F32, name="prod")
        out_rows = out.rearrange("(q t i) n -> t q i n", t=PACK, i=8)

        def multiply(t):
            for c, sl in enumerate(pieces):
                nc.scalar.copy(b_win[t][:, sl], b_acc[c, t])
            for acc, t0, per_bank, sl in b_banks:
                if t0 == t:
                    nc.scalar.activation(tanh_b[:, t0 : t0 + per_bank, sl], acc[:], ACT.Tanh)
            nc.vector.tensor_tensor(prod[:, t, :], b_win[t][:].indirect(n5_sb[:]), tanh_b[:, t, :], ALU.mult)

        def subtract_and_store(t):
            if t > 0:
                nc.scalar.copy(a_win[t][:, :S], a_acc[t][:])
            res = sb.tile([P, S], F32, name="res%d" % t)
            for c in halves:
                a4 = a4_first[:, cols(c)] if t == 0 else a_win[t][:].indirect(entries(n4_sb, c))
                nc.vector.tensor_tensor(res[:, cols(c)], a4, prod[:, t, cols(c)], ALU.subtract)
                nc.sync.dma_start(out_rows[t, :, :, cols(c)], res[:, cols(c)])

        multiply(0)
        for t in planes:
            if t + 1 < PACK:
                multiply(t + 1)
            subtract_and_store(t)
